import numpy as np
import ml_dtypes


def mxq(x, axis, fmt="e4m3"):
    dtype, down = {"e4m3": (ml_dtypes.float8_e4m3fn, 7), "e5m2": (ml_dtypes.float8_e5m2, 14)}[fmt]
    v = np.moveaxis(np.asarray(x, np.float32).astype(ml_dtypes.bfloat16).astype(np.float64), axis, -1)
    blocks = v.reshape(v.shape[:-1] + (-1, 32))
    amax = np.abs(blocks).max(-1, keepdims=True)
    byte = np.maximum(np.where(amax > 0, np.frexp(amax)[1] - 1 + 127, 0) - down, 1)
    scale = np.exp2(byte - 127.0)
    codes = (blocks / scale).astype(np.float32).astype(dtype).astype(np.float64)
    return np.moveaxis((codes * scale).reshape(v.shape), -1, axis)


WIDE = False


def mx_kscale(k):
    if not WIDE:
        return np.ones(k)
    levels = np.array([10, -10, 5, -5, 0])
    if k % 512:
        return np.exp2(np.random.permutation(np.resize(levels, k // 32))).repeat(32)
    a = np.empty((k // 512, 16))
    for p in range(k // 512):
        a[p, :8] = np.random.permutation(np.resize(levels, 8))
        for g in range(8):
            far = levels[np.abs(levels - a[p, g]) >= 10]
            a[p, g + 8] = far[np.random.randint(len(far))]
    return np.exp2(a.ravel()).repeat(32)


def f64(x):
    return np.asarray(x).astype(np.float64)


def striped(idx):
    return np.tile(idx.reshape(-1, 16).T, (8, 1)).astype(np.uint16)


def unstriped(offs):
    return offs[:16].T.reshape(-1).astype(np.int64)


def pack_weight(w):
    k, n = w.shape
    w = f64(np.asarray(w, np.float32).astype(ml_dtypes.bfloat16)).reshape(k // 32, 32, n)
    amax = np.abs(w).max(1)
    byte = np.clip(np.where(amax > 0, np.frexp(amax)[1] - 1 + 127 - 7, 1), 1, 254)
    scaled = (w * np.exp2(127.0 - byte)[:, None, :]).reshape(k, n).astype(np.float32)
    words = np.ascontiguousarray(scaled.reshape(k // 512, 128, 4, n).transpose(0, 1, 3, 2)).astype(ml_dtypes.float8_e4m3fn).view(np.uint8)
    return words, np.ascontiguousarray(byte.astype(np.uint8).reshape(k // 512, 16, n))


def unpack_weight(words, scales):
    g, p, n, _ = words.shape
    vals = np.ascontiguousarray(words).view(ml_dtypes.float8_e4m3fn).astype(np.float64) * np.repeat(np.exp2(scales.astype(np.float64) - 127.0), 8, axis=1)[..., None]
    return vals.transpose(0, 1, 3, 2).reshape(g * 512, n)


def sigmoid(v):
    return 1.0 / (1.0 + np.exp(-np.maximum(v, -700.0)))

def planes(y):
    n, m = y.shape
    v = y.astype(np.float32).astype(ml_dtypes.bfloat16).astype(np.float64).reshape(n // 32, 32, m)
    top = np.abs(v).max(1)
    byte = np.clip(np.where(top > 0, np.frexp(top)[1] - 1 + 127 - 7, 1), 1, 254)
    codes = (v * np.exp2(127.0 - byte)[:, None, :]).reshape(n, m).astype(np.float32).astype(ml_dtypes.float8_e4m3fn).view(np.uint8)
    words = codes.reshape(n // 512, 128, 4, m).transpose(0, 1, 3, 2)
    return np.ascontiguousarray(words), np.ascontiguousarray(byte.astype(np.uint8).reshape(n // 512, 16, m))


K, T, S, H, W, C = 512, 2048, 512, 512, 256, 512


def setup_inputs():
    n = np.random.standard_normal
    s = mx_kscale(K)[:, None]
    packed_xT = pack_weight(n((K, T)) * s)
    packed_w1 = pack_weight(n((K, H)) / np.sqrt(K) / s)
    perm = np.random.permutation(S)
    return {
        "x_words": packed_xT[0],
        "x_scales": packed_xT[1],
        "w1_words": packed_w1[0],
        "w1_scales": packed_w1[1],
        "gs": (np.random.uniform(0.5, 1.5, (K, 1)) / s).astype(np.float32),
        "wb": (n((K, S)) / np.sqrt(K) / s).astype(np.float32),
        "offs": striped(np.random.permutation(T)[:S]),
        "n1": striped(perm[:W]),
        "n2": striped(perm[W:]),
        "cand": striped(np.random.permutation(T)[:C]),
        "cb": striped(np.random.permutation(T)[:C]),
        "n3": striped(np.random.permutation(S)),
        "n4": striped(np.random.permutation(S)),
    }


def reference(x_words, x_scales, w1_words, w1_scales, gs, wb, offs, n1, n2, cand, cb, n3, n4):
    x_cand = unpack_weight(x_words, x_scales)[:, unstriped(cand)]
    xq = unpack_weight(x_words, x_scales)[:, unstriped(offs)]
    y = unpack_weight(w1_words, w1_scales).T @ xq
    pa = y[:, unstriped(n1)]
    pb = y[:, unstriped(n2)]
    ra = np.maximum(pa, pb)
    ds = y.copy()
    ds[:, unstriped(n1)] = ra
    z = f64(gs) * ds
    a = 0.0625 * ((x_cand.T @ mxq(z, 0, "e4m3")))
    x_cb = unpack_weight(x_words, x_scales)[:, unstriped(cb)]
    b = x_cb.T @ mxq(f64(wb), 0, "e4m3")
    out_0 = (a + a[:, unstriped(n3)]) * (sigmoid(b + b[:, unstriped(n4)]))
    return (out_0,) + planes(out_0)

@@ -1,0 +1,261 @@
+from contextlib import ExitStack
+
+import concourse.mybir as mybir
+from concourse.masks import make_identity
+
+F32 = mybir.dt.float32
+BF16 = mybir.dt.bfloat16
+I32 = mybir.dt.int32
+U32 = mybir.dt.uint32
+U16 = mybir.dt.uint16
+U8 = mybir.dt.uint8
+FP8X4 = mybir.dt.float8_e4m3fn_x4
+ACT = mybir.ActivationFunctionType
+ALU = mybir.AluOpType
+
+P = 128
+PACK = 4
+T = 2048
+S = 512
+W = 256
+HALF = S // 2
+QUARTER = S // 4
+FLOPS = 3 * 2 * 512 * 512 * 512
+
+
+def tile_picked_cdswtriebfill_none_po_kernel(
+    tc, x_words, x_scales, w1_words, w1_scales, gs, wb, offs, n1, n2, cand, cb, n3, n4, out_0, out_1, out_2
+):
+    nc = tc.nc
+    with ExitStack() as ctx:
+        keep = ctx.enter_context(tc.tile_pool(name="keep", bufs=1))
+        psum = ctx.enter_context(tc.psum_pool(name="psum", bufs=1))
+
+        def sbuf(name, shape, dtype):
+            return keep.tile(shape, dtype, name=name, align_bytes=64)
+
+        def bank(name, tag, shape):
+            return psum.tile(shape, F32, name=name, tag=tag)
+
+        def load_list(name, src):
+            tile = keep.tile(list(src.shape), U16, name=name)
+            nc.sync.dma_start(tile[:], src)
+            return tile
+
+        def load_scale_rows(queue, tile, src):
+            for q in range(4):
+                queue.dma_start(tile[32 * q : 32 * q + 4, :].bitcast(I32), src[0, 4 * q : 4 * q + 4, :].bitcast(I32))
+
+        x_w = sbuf("x_w", [P, T], I32)
+        x_s = sbuf("x_s", [P, T], U8)
+        w1_w = sbuf("w1_w", [P, S], I32)
+        w1_s = sbuf("w1_s", [P, S], U8)
+        nc.gpsimd.memset(x_s[:].bitcast(I32), 0)
+        nc.gpsimd.memset(w1_s[:].bitcast(I32), 0)
+        nc.sync.dma_start(w1_w[:], w1_words[0].rearrange("p c r -> p (c r)").bitcast(I32))
+        load_scale_rows(nc.sync, x_s, x_scales)
+        offs_t = load_list("offs_t", offs)
+        nc.sync.dma_start(x_w[:], x_words[0].rearrange("p c r -> p (c r)").bitcast(I32))
+        load_scale_rows(nc.sync, w1_s, w1_scales)
+        n1_t = load_list("n1_t", n1)
+        n2_t = load_list("n2_t", n2)
+        cb_t = load_list("cb_t", cb)
+        wb_raw = sbuf("wb_raw", [P, PACK, S], F32)
+        nc.sync.dma_start(wb_raw[:], wb.rearrange("(p j) w -> p j w", j=PACK))
+        cand_t = load_list("cand_t", cand)
+        gs_t = sbuf("gs_t", [P, PACK], F32)
+        nc.sync.dma_start(gs_t[:], gs.rearrange("(p t) o -> p (t o)", t=PACK))
+        n4_t = load_list("n4_t", n4)
+        n3_t = load_list("n3_t", n3)
+
+        ident = sbuf("ident", [P, P], F32)
+        make_identity(nc, ident[:])
+
+        def dealt(ap):
+            return ap.rearrange("p (t m) -> p m t", t=PACK)
+
+        def pick_words(name, lst, deal):
+            tile = sbuf(name, [P, S], U32)
+            nc.vector.tensor_copy(dealt(tile[:]) if deal else tile[:], x_w[:].bitcast(U32).indirect(lst[:]))
+            return tile
+
+        def pick_scales(name, lst, deal):
+            tile = sbuf(name, [P, S], U8)
+            nc.vector.tensor_copy(dealt(tile[:]) if deal else tile[:], x_s[:].indirect(lst[:]))
+            return tile
+
+        def product(out, l_w, l_s, t, r_w, r_s):
+            cols = slice(t * P, (t + 1) * P)
+            nc.tensor.matmul_mx(
+                out=out[:], lhsT=l_w[:, cols].bitcast(FP8X4), lhsT_scale=l_s[:, cols],
+                rhs=r_w[:].bitcast(FP8X4), rhs_scale=r_s[:], start=True, stop=True,
+            )
+
+        def interleave(dst, src, cols):
+            nc.vector.tensor_copy(
+                dst[:, cols, :].rearrange("p (c i) t -> p c t i", i=4),
+                src[:, :, cols].rearrange("p t (c i) -> p c t i", i=4),
+            )
+
+        def quantize(words, scales, grouped, cols):
+            nc.vector.quantize_mx(
+                out=words[:, cols].bitcast(FP8X4), scales=scales[:, cols],
+                in_=grouped[:, cols, :].rearrange("p c t -> p (c t)"),
+            )
+
+        xq_s = pick_scales("xq_s", offs_t, False)
+        w1d_w = sbuf("w1d_w", [P, S], I32)
+        nc.vector.tensor_copy(dealt(w1d_w[:]), w1_w[:].rearrange("p (m t) -> p m t", t=PACK))
+        xq_w = pick_words("xq_w", offs_t, False)
+        w1d_s = sbuf("w1d_s", [P, S], U8)
+        nc.vector.tensor_copy(dealt(w1d_s[:]), w1_s[:].rearrange("p (m t) -> p m t", t=PACK))
+
+        y_ps = [bank("y_ps%d" % t, "g%d" % t, [P, S]) for t in range(PACK)]
+        for t in range(PACK):
+            product(y_ps[t], w1d_w, w1d_s, t, xq_w, xq_s)
+
+        y = [sbuf("y%d" % t, [P, S], F32) for t in range(PACK)]
+        pa = sbuf("pa", [P, PACK, W], F32)
+        pb = sbuf("pb", [P, PACK, W], F32)
+        ra = sbuf("ra", [P, PACK, W], F32)
+        z_rows = sbuf("z_rows", [P, PACK, S], BF16)
+
+        def fetch_n1(t, on_scalar):
+            if on_scalar:
+                nc.scalar.activation(y[t][:], y_ps[t][:], ACT.Copy)
+            else:
+                nc.vector.tensor_copy(y[t][:], y_ps[t][:])
+            nc.scalar.activation(pa[:, t, :], y[t][:].indirect(n1_t[:]), ACT.Copy)
+
+        def larger(t):
+            nc.vector.tensor_copy(pb[:, t, :], y[t][:].indirect(n2_t[:]))
+            nc.vector.tensor_tensor(ra[:, t, :], pa[:, t, :], pb[:, t, :], ALU.max)
+
+        def put_n1(t):
+            nc.scalar.activation(y[t][:].indirect(n1_t[:]), ra[:, t, :], ACT.Copy)
+
+        def weigh(t, cols):
+            nc.vector.tensor_scalar(z_rows[:, t, cols], y[t][:, cols], gs_t[:, t : t + 1], None, ALU.mult)
+
+        whole = slice(0, S)
+        halves = [slice(h * HALF, (h + 1) * HALF) for h in range(2)]
+        quarters = [slice(q * QUARTER, (q + 1) * QUARTER) for q in range(4)]
+
+        b = [sbuf("b%d" % t, [P, S], F32) for t in range(PACK)]
+        b4 = [sbuf("b4_%d" % t, [P, S], F32) for t in range(PACK)]
+        b_ps = {}
+        sum_ps = {}
+        tanh_t = [sbuf("tanh_t%d" % t, [P, S], F32) for t in range(PACK)]
+        gate_ps = {}
+
+        def b_product(t):
+            b_ps[t] = bank("b_ps%d" % t, "s%d" % t, [P, S])
+            product(b_ps[t], cb_w, cb_s, t, wb_w, wb_s)
+
+        def b_copy(t, on_scalar):
+            if on_scalar:
+                nc.scalar.activation(b[t][:], b_ps[t][:], ACT.Copy)
+            else:
+                nc.vector.tensor_copy(b[t][:], b_ps[t][:])
+
+        def fetch_n4(t, on_scalar):
+            for h in range(2):
+                window = b[t][:].indirect(n4_t[:, 16 * h : 16 * h + 16])
+                if on_scalar:
+                    nc.scalar.activation(b4[t][:, halves[h]], window, ACT.Copy)
+                else:
+                    nc.vector.tensor_copy(b4[t][:, halves[h]], window)
+            sum_ps[t] = bank("sum_ps%d" % t, "s%d" % t, [P, S])
+            for q in range(4):
+                nc.tensor.matmul(sum_ps[t][:, quarters[q]], b[t][:, quarters[q]], ident[:], start=True, stop=False, is_transpose=True)
+                nc.tensor.matmul(sum_ps[t][:, quarters[q]], b4[t][:, quarters[q]], ident[:], start=False, stop=True, is_transpose=True)
+
+        def gate(t):
+            nc.scalar.activation(tanh_t[t][:], sum_ps[t][:], ACT.Tanh, scale=0.5)
+            gate_ps[t] = bank("gate_ps%d" % t, "s%d" % t, [P, S])
+            for q in range(4):
+                nc.tensor.transpose(gate_ps[t][:, quarters[q]], tanh_t[t][:, quarters[q]], ident[:])
+
+        wb_g = sbuf("wb_g", [P, S, PACK], BF16)
+        wb_w = sbuf("wb_w", [P, S], U32)
+        wb_s = sbuf("wb_s", [P, S], U8)
+        z_g = sbuf("z_g", [P, S, PACK], BF16)
+        z_w = sbuf("z_w", [P, S], U32)
+        z_s = sbuf("z_s", [P, S], U8)
+        a = [sbuf("a%d" % t, [P, S], F32) for t in range(PACK)]
+        a3 = [sbuf("a3_%d" % t, [P, S], F32) for t in range(PACK)]
+        a_ps = {}
+        both = [sbuf("both%d" % t, [P, S], F32) for t in range(PACK)]
+        res = sbuf("res", [P, PACK, S], F32)
+        res_g = sbuf("res_g", [P, S, PACK], BF16)
+        res_w = sbuf("res_w", [P, S], I32)
+        res_s = sbuf("res_s", [P, S], U8)
+        out_rows = out_0.rearrange("(p t) j -> p t j", t=PACK)
+        out_words = out_1[0].rearrange("p c r -> p (c r)").bitcast(I32)
+
+        def a_product(t):
+            a_ps[t] = bank("a_ps%d" % t, "g%d" % t, [P, S])
+            product(a_ps[t], cand_w, cand_s, t, z_w, z_s)
+
+        def a_copy(t, on_scalar):
+            if on_scalar:
+                nc.scalar.activation(a[t][:], a_ps[t][:], ACT.Copy, scale=0.03125)
+            else:
+                nc.vector.tensor_scalar(a[t][:], a_ps[t][:], 0.03125, None, ALU.mult)
+
+        def fetch_n3(t, h):
+            nc.scalar.activation(a3[t][:, halves[h]], a[t][:].indirect(n3_t[:, 16 * h : 16 * h + 16]), ACT.Copy)
+
+        def finish(t, cols):
+            nc.vector.tensor_tensor(both[t][:, cols], a[t][:, cols], a3[t][:, cols], ALU.add)
+            nc.vector.scalar_tensor_tensor(res[:, t, cols], gate_ps[t][:, cols], 1.0, both[t][:, cols], ALU.add, ALU.mult)
+
+        def store(t):
+            nc.sync.dma_start(out_rows[:, t, :], res[:, t, :])
+
+        def planes(cols):
+            interleave(res_g, res, cols)
+            quantize(res_w, res_s, res_g, cols)
+            nc.sync.dma_start(out_words[:, cols], res_w[:, cols])
+
+        for t in range(PACK):
+            fetch_n1(t, True)
+            larger(t)
+        for t in range(PACK):
+            put_n1(t)
+        cb_s = pick_scales("cb_s", cb_t, True)
+        cb_w = pick_words("cb_w", cb_t, True)
+        interleave(wb_g, wb_raw, whole)
+        cand_s = pick_scales("cand_s", cand_t, True)
+        quantize(wb_w, wb_s, wb_g, whole)
+        cand_w = pick_words("cand_w", cand_t, True)
+        for t in range(PACK):
+            b_product(t)
+            b_copy(t, True)
+        for t in range(3):
+            weigh(t, whole)
+        for cols in halves:
+            weigh(3, cols)
+        for cols in halves:
+            interleave(z_g, z_rows, cols)
+        for cols in halves:
+            quantize(z_w, z_s, z_g, cols)
+        for t in range(PACK):
+            a_product(t)
+        for t in range(PACK):
+            a_copy(t, t>=2)
+            fetch_n4(t, t<2)
+            gate(t)
+            fetch_n3(t, 0)
+            fetch_n3(t, 1)
+            if t < 3:
+                finish(t, whole)
+                store(t)
+        for cols in halves:
+            finish(3, cols)
+        store(3)
+        for cols in halves:
+            planes(cols)
+        for q in range(4):
+            queue = nc.sync if q % 2 else nc.scalar
+            queue.dma_start(out_2[0, 4 * q : 4 * q + 4, :].bitcast(I32), res_s[32 * q : 32 * q + 4, :].bitcast(I32))

@@ -31,8 +31,8 @@ def tile_picked_cdswtriebfill_none_po_kernel(
         keep = ctx.enter_context(tc.tile_pool(name="keep", bufs=1))
         psum = ctx.enter_context(tc.psum_pool(name="psum", bufs=1))
 
-        def sbuf(name, shape, dtype):
-            return keep.tile(shape, dtype, name=name, align_bytes=64)
+        def sbuf(name, shape, dtype, tag=""):
+            return keep.tile(shape, dtype, name=name, tag=tag, align_bytes=64)
 
         def bank(name, tag, shape):
             return psum.tile(shape, F32, name=name, tag=tag)
@@ -50,22 +50,23 @@ def tile_picked_cdswtriebfill_none_po_kernel(
         x_s = sbuf("x_s", [P, T], U8)
         w1_w = sbuf("w1_w", [P, S], I32)
         w1_s = sbuf("w1_s", [P, S], U8)
-        nc.gpsimd.memset(x_s[:].bitcast(I32), 0)
+        nc.gpsimd.memset(x_s[:, : T // 2].bitcast(I32), 0)
+        nc.vector.memset(x_s[:, T // 2 :].bitcast(I32), 0)
         nc.gpsimd.memset(w1_s[:].bitcast(I32), 0)
-        nc.sync.dma_start(w1_w[:], w1_words[0].rearrange("p c r -> p (c r)").bitcast(I32))
-        load_scale_rows(nc.sync, x_s, x_scales)
         offs_t = load_list("offs_t", offs)
-        nc.sync.dma_start(x_w[:], x_words[0].rearrange("p c r -> p (c r)").bitcast(I32))
+        nc.scalar.dma_start(w1_w[:], w1_words[0].rearrange("p c r -> p (c r)").bitcast(I32))
+        gs_t = sbuf("gs_t", [P, PACK], F32)
+        nc.scalar.dma_start(gs_t[:], gs.rearrange("(p t) o -> p (t o)", t=PACK))
+        nc.scalar.dma_start(x_w[:], x_words[0].rearrange("p c r -> p (c r)").bitcast(I32))
+        load_scale_rows(nc.sync, x_s, x_scales)
         load_scale_rows(nc.sync, w1_s, w1_scales)
         n1_t = load_list("n1_t", n1)
-        n2_t = load_list("n2_t", n2)
         cb_t = load_list("cb_t", cb)
         wb_raw = sbuf("wb_raw", [P, PACK, S], F32)
         nc.sync.dma_start(wb_raw[:], wb.rearrange("(p j) w -> p j w", j=PACK))
-        cand_t = load_list("cand_t", cand)
-        gs_t = sbuf("gs_t", [P, PACK], F32)
-        nc.sync.dma_start(gs_t[:], gs.rearrange("(p t) o -> p (t o)", t=PACK))
+        n2_t = load_list("n2_t", n2)
         n4_t = load_list("n4_t", n4)
+        cand_t = load_list("cand_t", cand)
         n3_t = load_list("n3_t", n3)
 
         ident = sbuf("ident", [P, P], F32)
@@ -75,12 +76,12 @@ def tile_picked_cdswtriebfill_none_po_kernel(
             return ap.rearrange("p (t m) -> p m t", t=PACK)
 
         def pick_words(name, lst, deal):
-            tile = sbuf(name, [P, S], U32)
+            tile = sbuf(name, [P, S], U32, "dealt_w" if deal else "")
             nc.vector.tensor_copy(dealt(tile[:]) if deal else tile[:], x_w[:].bitcast(U32).indirect(lst[:]))
             return tile
 
         def pick_scales(name, lst, deal):
-            tile = sbuf(name, [P, S], U8)
+            tile = sbuf(name, [P, S], U8, "dealt_s" if deal else "")
             nc.vector.tensor_copy(dealt(tile[:]) if deal else tile[:], x_s[:].indirect(lst[:]))
             return tile
 
@@ -117,8 +118,8 @@ def tile_picked_cdswtriebfill_none_po_kernel(
         y = [sbuf("y%d" % t, [P, S], F32) for t in range(PACK)]
         pa = sbuf("pa", [P, PACK, W], F32)
         pb = sbuf("pb", [P, PACK, W], F32)
-        ra = sbuf("ra", [P, PACK, W], F32)
-        z_rows = sbuf("z_rows", [P, PACK, S], BF16)
+        ra = sbuf("ra", [P, PACK, W], F32, "rows")
+        z_rows = sbuf("z_rows", [P, PACK, S], BF16, "late")
 
         def fetch_n1(t, on_scalar):
             if on_scalar:
@@ -135,14 +136,17 @@ def tile_picked_cdswtriebfill_none_po_kernel(
             nc.scalar.activation(y[t][:].indirect(n1_t[:]), ra[:, t, :], ACT.Copy)
 
         def weigh(t, cols):
-            nc.vector.tensor_scalar(z_rows[:, t, cols], y[t][:, cols], gs_t[:, t : t + 1], None, ALU.mult)
+            if t<3:
+                nc.gpsimd.tensor_scalar(z_rows[:, t, cols], y[t][:, cols], gs_t[:, t : t + 1], 0.0, ALU.mult, ALU.add)
+            else:
+                nc.vector.tensor_scalar(z_rows[:, t, cols], y[t][:, cols], gs_t[:, t : t + 1], None, ALU.mult)
 
         whole = slice(0, S)
         halves = [slice(h * HALF, (h + 1) * HALF) for h in range(2)]
         quarters = [slice(q * QUARTER, (q + 1) * QUARTER) for q in range(4)]
 
-        b = [sbuf("b%d" % t, [P, S], F32) for t in range(PACK)]
-        b4 = [sbuf("b4_%d" % t, [P, S], F32) for t in range(PACK)]
+        b = {}
+        b4 = {t: sbuf("b4_%d" % t, [P, S], F32, "fetched%d" % t) for t in range(2)}
         b_ps = {}
         sum_ps = {}
         tanh_t = [sbuf("tanh_t%d" % t, [P, S], F32) for t in range(PACK)]
@@ -153,14 +157,23 @@ def tile_picked_cdswtriebfill_none_po_kernel(
             product(b_ps[t], cb_w, cb_s, t, wb_w, wb_s)
 
         def b_copy(t, on_scalar):
-            if on_scalar:
-                nc.scalar.activation(b[t][:], b_ps[t][:], ACT.Copy)
+            if t < 2:
+                b[t] = sbuf("b%d" % t, [P, S], F32)[:]
             else:
-                nc.vector.tensor_copy(b[t][:], b_ps[t][:])
+                if t == 2:
+                    b["late"] = sbuf("b_late", [P, PACK - 2, S], F32, "rows")
+                b[t] = b["late"][:, t - 2, :]
+            if on_scalar:
+                nc.scalar.activation(b[t], b_ps[t][:], ACT.Copy)
+            else:
+                nc.vector.tensor_copy(b[t], b_ps[t][:])
 
         def fetch_n4(t, on_scalar):
+            if t == 2:
+                b4_late = sbuf("b4_late", [P, 2, S], F32, "late")
+                b4[2], b4[3] = b4_late[:, 0, :], b4_late[:, 1, :]
             for h in range(2):
-                window = b[t][:].indirect(n4_t[:, 16 * h : 16 * h + 16])
+                window = b[t].indirect(n4_t[:, 16 * h : 16 * h + 16])
                 if on_scalar:
                     nc.scalar.activation(b4[t][:, halves[h]], window, ACT.Copy)
                 else:
@@ -172,7 +185,9 @@ def tile_picked_cdswtriebfill_none_po_kernel(
 
         def gate(t):
             nc.scalar.activation(tanh_t[t][:], sum_ps[t][:], ACT.Tanh, scale=0.5)
-            gate_ps[t] = bank("gate_ps%d" % t, "s%d" % t, [P, S])
+
+        def turn_back(t):
+            gate_ps[t] = bank("gate_ps%d" % t, "g%d" % t, [P, S])
             for q in range(4):
                 nc.tensor.transpose(gate_ps[t][:, quarters[q]], tanh_t[t][:, quarters[q]], ident[:])
 
@@ -183,7 +198,7 @@ def tile_picked_cdswtriebfill_none_po_kernel(
         z_w = sbuf("z_w", [P, S], U32)
         z_s = sbuf("z_s", [P, S], U8)
         a = [sbuf("a%d" % t, [P, S], F32) for t in range(PACK)]
-        a3 = [sbuf("a3_%d" % t, [P, S], F32) for t in range(PACK)]
+        a3 = {}
         a_ps = {}
         both = [sbuf("both%d" % t, [P, S], F32) for t in range(PACK)]
         res = sbuf("res", [P, PACK, S], F32)
@@ -204,10 +219,15 @@ def tile_picked_cdswtriebfill_none_po_kernel(
                 nc.vector.tensor_scalar(a[t][:], a_ps[t][:], 0.03125, None, ALU.mult)
 
         def fetch_n3(t, h):
+            if h == 0 and t < 2:
+                a3[t] = sbuf("a3_%d" % t, [P, S], F32, "fetched%d" % t)
+            if h == 0 and t == 2:
+                a3["late"] = sbuf("a3_late", [P, 2, S], F32, "late")
+                a3[2], a3[3] = a3["late"][:, 0, :], a3["late"][:, 1, :]
             nc.scalar.activation(a3[t][:, halves[h]], a[t][:].indirect(n3_t[:, 16 * h : 16 * h + 16]), ACT.Copy)
 
         def finish(t, cols):
-            nc.vector.tensor_tensor(both[t][:, cols], a[t][:, cols], a3[t][:, cols], ALU.add)
+            (nc.gpsimd if t<2 else nc.vector).tensor_tensor(both[t][:, cols], a[t][:, cols], a3[t][:, cols], ALU.add)
             nc.vector.scalar_tensor_tensor(res[:, t, cols], gate_ps[t][:, cols], 1.0, both[t][:, cols], ALU.add, ALU.mult)
 
         def store(t):
@@ -225,13 +245,20 @@ def tile_picked_cdswtriebfill_none_po_kernel(
             put_n1(t)
         cb_s = pick_scales("cb_s", cb_t, True)
         cb_w = pick_words("cb_w", cb_t, True)
-        interleave(wb_g, wb_raw, whole)
-        cand_s = pick_scales("cand_s", cand_t, True)
+        nc.gpsimd.tensor_scalar(wb_g[:], wb_raw[:].rearrange("p t c -> p c t"), 1.0, 0.0, ALU.mult, ALU.add)
         quantize(wb_w, wb_s, wb_g, whole)
-        cand_w = pick_words("cand_w", cand_t, True)
         for t in range(PACK):
             b_product(t)
+        b_copy(0, False)
+        b_copy(1, False)
+        fetch_n4(0, False)
+        cand_s = pick_scales("cand_s", cand_t, True)
+        cand_w = pick_words("cand_w", cand_t, True)
+        gate(0)
+
+        for t in range(2, PACK):
             b_copy(t, True)
+        fetch_n4(1, True)
         for t in range(3):
             weigh(t, whole)
         for cols in halves:
@@ -243,9 +270,15 @@ def tile_picked_cdswtriebfill_none_po_kernel(
         for t in range(PACK):
             a_product(t)
         for t in range(PACK):
-            a_copy(t, t>=2)
-            fetch_n4(t, t<2)
-            gate(t)
+            a_copy(t, t==0)
+            if t == 0:
+                turn_back(0)
+            if t < 2:
+                fetch_n4(t + 2, False)
+        for t in range(PACK):
+            if t > 0:
+                gate(t)
+                turn_back(t)
             fetch_n3(t, 0)
             fetch_n3(t, 1)
             if t < 3:

@@ -61,12 +61,12 @@ def tile_picked_cdswtriebfill_none_po_kernel(
         load_scale_rows(nc.sync, x_s, x_scales)
         load_scale_rows(nc.sync, w1_s, w1_scales)
         n1_t = load_list("n1_t", n1)
+        n2_t = load_list("n2_t", n2)
         cb_t = load_list("cb_t", cb)
         wb_raw = sbuf("wb_raw", [P, PACK, S], F32)
         nc.sync.dma_start(wb_raw[:], wb.rearrange("(p j) w -> p j w", j=PACK))
-        n2_t = load_list("n2_t", n2)
-        n4_t = load_list("n4_t", n4)
         cand_t = load_list("cand_t", cand)
+        n4_t = load_list("n4_t", n4)
         n3_t = load_list("n3_t", n3)
 
         ident = sbuf("ident", [P, P], F32)
@@ -76,12 +76,12 @@ def tile_picked_cdswtriebfill_none_po_kernel(
             return ap.rearrange("p (t m) -> p m t", t=PACK)
 
         def pick_words(name, lst, deal):
-            tile = sbuf(name, [P, S], U32, "dealt_w" if deal else "")
+            tile = sbuf(name, [P, S], U32, "")
             nc.vector.tensor_copy(dealt(tile[:]) if deal else tile[:], x_w[:].bitcast(U32).indirect(lst[:]))
             return tile
 
         def pick_scales(name, lst, deal):
-            tile = sbuf(name, [P, S], U8, "dealt_s" if deal else "")
+            tile = sbuf(name, [P, S], U8, "")
             nc.vector.tensor_copy(dealt(tile[:]) if deal else tile[:], x_s[:].indirect(lst[:]))
             return tile
 
@@ -119,7 +119,7 @@ def tile_picked_cdswtriebfill_none_po_kernel(
         pa = sbuf("pa", [P, PACK, W], F32)
         pb = sbuf("pb", [P, PACK, W], F32)
         ra = sbuf("ra", [P, PACK, W], F32, "rows")
-        z_rows = sbuf("z_rows", [P, PACK, S], BF16, "late")
+        z_pairs = sbuf("z_pairs", [P, 2, S, 2], BF16, "late")
 
         def fetch_n1(t, on_scalar):
             if on_scalar:
@@ -136,10 +136,7 @@ def tile_picked_cdswtriebfill_none_po_kernel(
             nc.scalar.activation(y[t][:].indirect(n1_t[:]), ra[:, t, :], ACT.Copy)
 
         def weigh(t, cols):
-            if t<3:
-                nc.gpsimd.tensor_scalar(z_rows[:, t, cols], y[t][:, cols], gs_t[:, t : t + 1], 0.0, ALU.mult, ALU.add)
-            else:
-                nc.vector.tensor_scalar(z_rows[:, t, cols], y[t][:, cols], gs_t[:, t : t + 1], None, ALU.mult)
+            nc.vector.tensor_scalar(z_pairs[:, t // 2, cols, t % 2], y[t][:, cols], gs_t[:, t : t + 1], None, ALU.mult)
 
         whole = slice(0, S)
         halves = [slice(h * HALF, (h + 1) * HALF) for h in range(2)]
@@ -233,8 +230,12 @@ def tile_picked_cdswtriebfill_none_po_kernel(
         def store(t):
             nc.sync.dma_start(out_rows[:, t, :], res[:, t, :])
 
+        def round_pair(u, cols):
+            pair = slice(2 * u, 2 * u + 2)
+            nc.vector.tensor_copy(res_g[:, cols, pair], res[:, pair, cols].rearrange("p t c -> p c t"))
+
         def planes(cols):
-            interleave(res_g, res, cols)
+            round_pair(1, cols)
             quantize(res_w, res_s, res_g, cols)
             nc.sync.dma_start(out_words[:, cols], res_w[:, cols])
 
@@ -245,36 +246,39 @@ def tile_picked_cdswtriebfill_none_po_kernel(
             put_n1(t)
         cb_s = pick_scales("cb_s", cb_t, True)
         cb_w = pick_words("cb_w", cb_t, True)
-        nc.gpsimd.tensor_scalar(wb_g[:], wb_raw[:].rearrange("p t c -> p c t"), 1.0, 0.0, ALU.mult, ALU.add)
+        interleave(wb_g, wb_raw, whole)
         quantize(wb_w, wb_s, wb_g, whole)
         for t in range(PACK):
             b_product(t)
-        b_copy(0, False)
-        b_copy(1, False)
-        fetch_n4(0, False)
         cand_s = pick_scales("cand_s", cand_t, True)
         cand_w = pick_words("cand_w", cand_t, True)
-        gate(0)
-
+        for t in range(2):
+            b_copy(t, False)
         for t in range(2, PACK):
             b_copy(t, True)
-        fetch_n4(1, True)
         for t in range(3):
             weigh(t, whole)
         for cols in halves:
             weigh(3, cols)
         for cols in halves:
-            interleave(z_g, z_rows, cols)
+            nc.vector.tensor_copy(
+                z_g[:, cols, :].bitcast(I32),
+                z_pairs[:, :, cols, :].bitcast(I32).rearrange("p u c o -> p c (u o)"),
+            )
         for cols in halves:
             quantize(z_w, z_s, z_g, cols)
+        fetch_n4(0, True)
+        gate(0)
+
         for t in range(PACK):
             a_product(t)
         for t in range(PACK):
-            a_copy(t, t==0)
+            a_copy(t, t<2)
             if t == 0:
                 turn_back(0)
-            if t < 2:
-                fetch_n4(t + 2, False)
+                fetch_n4(1, False)
+            if t in (0, 1):
+                fetch_n4((0, 1).index(t) + 2, False)
         for t in range(PACK):
             if t > 0:
                 gate(t)
@@ -284,6 +288,7 @@ def tile_picked_cdswtriebfill_none_po_kernel(
             if t < 3:
                 finish(t, whole)
                 store(t)
+        nc.scalar.copy(res_g[:, :, 0:2], res[:, 0:2, :].rearrange("p t c -> p c t"))
         for cols in halves:
             finish(3, cols)
         store(3)

@@ -18,8 +18,12 @@ PACK = 4
 T = 2048
 S = 512
 W = 256
-HALF = S // 2
-QUARTER = S // 4
+LIST_HALF = 16
+SPARE = 16
+A_SCALE = 0.0625 * 0.5
+LAST = PACK - 1
+A_ON_SCALAR = 2
+ADD_ON_GPSIMD = 2
 FLOPS = 3 * 2 * 512 * 512 * 512
 
 
@@ -27,45 +31,51 @@ def tile_picked_cdswtriebfill_none_po_kernel(
     tc, x_words, x_scales, w1_words, w1_scales, gs, wb, offs, n1, n2, cand, cb, n3, n4, out_0, out_1, out_2
 ):
     nc = tc.nc
+    whole = slice(0, S)
+    halves = [slice(h * W, (h + 1) * W) for h in range(2)]
+    quarters = [slice(q * P, (q + 1) * P) for q in range(4)]
+
     with ExitStack() as ctx:
         keep = ctx.enter_context(tc.tile_pool(name="keep", bufs=1))
         psum = ctx.enter_context(tc.psum_pool(name="psum", bufs=1))
 
-        def sbuf(name, shape, dtype, tag=""):
-            return keep.tile(shape, dtype, name=name, tag=tag, align_bytes=64)
+        def sbuf(name, shape, dtype, buffer=""):
+            return keep.tile(shape, dtype, name=name, tag=buffer, align_bytes=64)
 
-        def bank(name, tag, shape):
-            return psum.tile(shape, F32, name=name, tag=tag)
+        def bank(name, side, t):
+            return psum.tile([P, S], F32, name="%s%d" % (name, t), tag="%s%d" % (side, t))
 
         def load_list(name, src):
             tile = keep.tile(list(src.shape), U16, name=name)
             nc.sync.dma_start(tile[:], src)
             return tile
 
-        def load_scale_rows(queue, tile, src):
+        def load_words(tile, src):
+            nc.sync.dma_start(tile[:], src[0].rearrange("p c r -> p (c r)").bitcast(I32))
+
+        def load_scale_rows(tile, src):
             for q in range(4):
-                queue.dma_start(tile[32 * q : 32 * q + 4, :].bitcast(I32), src[0, 4 * q : 4 * q + 4, :].bitcast(I32))
+                nc.sync.dma_start(tile[32 * q : 32 * q + 4, :].bitcast(I32), src[0, 4 * q : 4 * q + 4, :].bitcast(I32))
 
         x_w = sbuf("x_w", [P, T], I32)
         x_s = sbuf("x_s", [P, T], U8)
         w1_w = sbuf("w1_w", [P, S], I32)
-        w1_s = sbuf("w1_s", [P, S], U8)
-        nc.gpsimd.memset(x_s[:, : T // 2].bitcast(I32), 0)
-        nc.vector.memset(x_s[:, T // 2 :].bitcast(I32), 0)
+        w1_s = sbuf("w1_s", [P, S], U8, "w1_scales_then_cb_words")
+        nc.gpsimd.memset(x_s[:].bitcast(I32), 0)
         nc.gpsimd.memset(w1_s[:].bitcast(I32), 0)
+        load_words(w1_w, w1_words)
+        load_scale_rows(x_s, x_scales)
         offs_t = load_list("offs_t", offs)
-        nc.scalar.dma_start(w1_w[:], w1_words[0].rearrange("p c r -> p (c r)").bitcast(I32))
-        gs_t = sbuf("gs_t", [P, PACK], F32)
-        nc.scalar.dma_start(gs_t[:], gs.rearrange("(p t) o -> p (t o)", t=PACK))
-        nc.scalar.dma_start(x_w[:], x_words[0].rearrange("p c r -> p (c r)").bitcast(I32))
-        load_scale_rows(nc.sync, x_s, x_scales)
-        load_scale_rows(nc.sync, w1_s, w1_scales)
-        n1_t = load_list("n1_t", n1)
-        n2_t = load_list("n2_t", n2)
         cb_t = load_list("cb_t", cb)
+        load_words(x_w, x_words)
+        load_scale_rows(w1_s, w1_scales)
+        n1_t = load_list("n1_t", n1)
         wb_raw = sbuf("wb_raw", [P, PACK, S], F32)
         nc.sync.dma_start(wb_raw[:], wb.rearrange("(p j) w -> p j w", j=PACK))
+        n2_t = load_list("n2_t", n2)
         cand_t = load_list("cand_t", cand)
+        gs_t = sbuf("gs_t", [P, PACK], F32)
+        nc.sync.dma_start(gs_t[:], gs.rearrange("(p t) o -> p (t o)", t=PACK))
         n4_t = load_list("n4_t", n4)
         n3_t = load_list("n3_t", n3)
 
@@ -75,225 +85,186 @@ def tile_picked_cdswtriebfill_none_po_kernel(
         def dealt(ap):
             return ap.rearrange("p (t m) -> p m t", t=PACK)
 
-        def pick_words(name, lst, deal):
-            tile = sbuf(name, [P, S], U32, "")
-            nc.vector.tensor_copy(dealt(tile[:]) if deal else tile[:], x_w[:].bitcast(U32).indirect(lst[:]))
+        def deal(name, src, dtype):
+            tile = sbuf(name, [P, S], dtype)
+            nc.vector.tensor_copy(dealt(tile[:]), src[:].rearrange("p (m t) -> p m t", t=PACK))
             return tile
 
-        def pick_scales(name, lst, deal):
-            tile = sbuf(name, [P, S], U8, "")
-            nc.vector.tensor_copy(dealt(tile[:]) if deal else tile[:], x_s[:].indirect(lst[:]))
+        def pick_words(name, picks, stationary, buffer=""):
+            tile = sbuf(name, [P, S], U32, buffer)
+            nc.vector.tensor_copy(dealt(tile[:]) if stationary else tile[:], x_w[:].bitcast(U32).indirect(picks[:]))
             return tile
 
-        def product(out, l_w, l_s, t, r_w, r_s):
-            cols = slice(t * P, (t + 1) * P)
+        def pick_scales(name, picks, stationary):
+            tile = sbuf(name, [P, S], U8)
+            nc.vector.tensor_copy(dealt(tile[:]) if stationary else tile[:], x_s[:].indirect(picks[:]))
+            return tile
+
+        def product(out, t, left_w, left_s, right_w, right_s):
             nc.tensor.matmul_mx(
-                out=out[:], lhsT=l_w[:, cols].bitcast(FP8X4), lhsT_scale=l_s[:, cols],
-                rhs=r_w[:].bitcast(FP8X4), rhs_scale=r_s[:], start=True, stop=True,
-            )
-
-        def interleave(dst, src, cols):
-            nc.vector.tensor_copy(
-                dst[:, cols, :].rearrange("p (c i) t -> p c t i", i=4),
-                src[:, :, cols].rearrange("p t (c i) -> p c t i", i=4),
+                out=out[:],
+                lhsT=left_w[:, quarters[t]].bitcast(FP8X4),
+                lhsT_scale=left_s[:, quarters[t]],
+                rhs=right_w[:].bitcast(FP8X4),
+                rhs_scale=right_s[:],
+                start=True,
+                stop=True,
             )
 
         def quantize(words, scales, grouped, cols):
             nc.vector.quantize_mx(
-                out=words[:, cols].bitcast(FP8X4), scales=scales[:, cols],
+                out=words[:, cols].bitcast(FP8X4),
+                scales=scales[:, cols],
                 in_=grouped[:, cols, :].rearrange("p c t -> p (c t)"),
             )
 
         xq_s = pick_scales("xq_s", offs_t, False)
-        w1d_w = sbuf("w1d_w", [P, S], I32)
-        nc.vector.tensor_copy(dealt(w1d_w[:]), w1_w[:].rearrange("p (m t) -> p m t", t=PACK))
+        w1d_w = deal("w1d_w", w1_w, I32)
+        cb_s = pick_scales("cb_s", cb_t, True)
         xq_w = pick_words("xq_w", offs_t, False)
-        w1d_s = sbuf("w1d_s", [P, S], U8)
-        nc.vector.tensor_copy(dealt(w1d_s[:]), w1_s[:].rearrange("p (m t) -> p m t", t=PACK))
-
-        y_ps = [bank("y_ps%d" % t, "g%d" % t, [P, S]) for t in range(PACK)]
+        w1d_s = deal("w1d_s", w1_s, U8)
+        y_ps = [bank("y_ps", "left", t) for t in range(PACK)]
         for t in range(PACK):
-            product(y_ps[t], w1d_w, w1d_s, t, xq_w, xq_s)
+            product(y_ps[t], t, w1d_w, w1d_s, xq_w, xq_s)
 
         y = [sbuf("y%d" % t, [P, S], F32) for t in range(PACK)]
         pa = sbuf("pa", [P, PACK, W], F32)
         pb = sbuf("pb", [P, PACK, W], F32)
-        ra = sbuf("ra", [P, PACK, W], F32, "rows")
-        z_pairs = sbuf("z_pairs", [P, 2, S, 2], BF16, "late")
-
-        def fetch_n1(t, on_scalar):
-            if on_scalar:
-                nc.scalar.activation(y[t][:], y_ps[t][:], ACT.Copy)
-            else:
-                nc.vector.tensor_copy(y[t][:], y_ps[t][:])
+        ra = sbuf("ra", [P, PACK, W], F32, "ra_then_last_b")
+        for t in range(PACK):
+            nc.scalar.activation(y[t][:], y_ps[t][:], ACT.Copy)
             nc.scalar.activation(pa[:, t, :], y[t][:].indirect(n1_t[:]), ACT.Copy)
-
-        def larger(t):
             nc.vector.tensor_copy(pb[:, t, :], y[t][:].indirect(n2_t[:]))
             nc.vector.tensor_tensor(ra[:, t, :], pa[:, t, :], pb[:, t, :], ALU.max)
-
-        def put_n1(t):
+        for t in range(PACK):
             nc.scalar.activation(y[t][:].indirect(n1_t[:]), ra[:, t, :], ACT.Copy)
+
+        cb_w = pick_words("cb_w", cb_t, True, "w1_scales_then_cb_words")
+        wb_g = sbuf("wb_g", [P, S, PACK], BF16)
+        wb_w = sbuf("wb_w", [P, S], U32)
+        wb_s = sbuf("wb_s", [P, S], U8)
+        nc.vector.tensor_copy(
+            wb_g[:].rearrange("p (c i) t -> p c t i", i=4), wb_raw[:].rearrange("p t (c i) -> p c t i", i=4)
+        )
+        quantize(wb_w, wb_s, wb_g, whole)
+        b_ps = [bank("b_ps", "right", t) for t in range(PACK)]
+        for t in range(PACK):
+            product(b_ps[t], t, cb_w, cb_s, wb_w, wb_s)
+        cand_s = pick_scales("cand_s", cand_t, True)
+        cand_w = pick_words("cand_w", cand_t, True)
+        b = [sbuf("b%d" % t, [P, S], F32) for t in range(LAST)]
+        for t in range(LAST):
+            nc.vector.tensor_copy(b[t][:], b_ps[t][:])
+        b.append(sbuf("b_last", [P, S], F32, "ra_then_last_b"))
+        nc.scalar.activation(b[LAST][:], b_ps[LAST][:], ACT.Copy)
+
+        z_pairs = sbuf("z_pairs", [P, 2, S, 2], BF16, "fetched1")
+        z_g = sbuf("z_g", [P, S, PACK], BF16, "fetched23")
+        z_w = sbuf("z_w", [P, S], U32)
+        z_s = sbuf("z_s", [P, S], U8)
 
         def weigh(t, cols):
             nc.vector.tensor_scalar(z_pairs[:, t // 2, cols, t % 2], y[t][:, cols], gs_t[:, t : t + 1], None, ALU.mult)
 
-        whole = slice(0, S)
-        halves = [slice(h * HALF, (h + 1) * HALF) for h in range(2)]
-        quarters = [slice(q * QUARTER, (q + 1) * QUARTER) for q in range(4)]
-
-        b = {}
-        b4 = {t: sbuf("b4_%d" % t, [P, S], F32, "fetched%d" % t) for t in range(2)}
-        b_ps = {}
-        sum_ps = {}
-        tanh_t = [sbuf("tanh_t%d" % t, [P, S], F32) for t in range(PACK)]
-        gate_ps = {}
-
-        def b_product(t):
-            b_ps[t] = bank("b_ps%d" % t, "s%d" % t, [P, S])
-            product(b_ps[t], cb_w, cb_s, t, wb_w, wb_s)
-
-        def b_copy(t, on_scalar):
-            if t < 2:
-                b[t] = sbuf("b%d" % t, [P, S], F32)[:]
-            else:
-                if t == 2:
-                    b["late"] = sbuf("b_late", [P, PACK - 2, S], F32, "rows")
-                b[t] = b["late"][:, t - 2, :]
-            if on_scalar:
-                nc.scalar.activation(b[t], b_ps[t][:], ACT.Copy)
-            else:
-                nc.vector.tensor_copy(b[t], b_ps[t][:])
-
-        def fetch_n4(t, on_scalar):
-            if t == 2:
-                b4_late = sbuf("b4_late", [P, 2, S], F32, "late")
-                b4[2], b4[3] = b4_late[:, 0, :], b4_late[:, 1, :]
-            for h in range(2):
-                window = b[t].indirect(n4_t[:, 16 * h : 16 * h + 16])
-                if on_scalar:
-                    nc.scalar.activation(b4[t][:, halves[h]], window, ACT.Copy)
-                else:
-                    nc.vector.tensor_copy(b4[t][:, halves[h]], window)
-            sum_ps[t] = bank("sum_ps%d" % t, "s%d" % t, [P, S])
-            for q in range(4):
-                nc.tensor.matmul(sum_ps[t][:, quarters[q]], b[t][:, quarters[q]], ident[:], start=True, stop=False, is_transpose=True)
-                nc.tensor.matmul(sum_ps[t][:, quarters[q]], b4[t][:, quarters[q]], ident[:], start=False, stop=True, is_transpose=True)
-
-        def gate(t):
-            nc.scalar.activation(tanh_t[t][:], sum_ps[t][:], ACT.Tanh, scale=0.5)
-
-        def turn_back(t):
-            gate_ps[t] = bank("gate_ps%d" % t, "g%d" % t, [P, S])
-            for q in range(4):
-                nc.tensor.transpose(gate_ps[t][:, quarters[q]], tanh_t[t][:, quarters[q]], ident[:])
-
-        wb_g = sbuf("wb_g", [P, S, PACK], BF16)
-        wb_w = sbuf("wb_w", [P, S], U32)
-        wb_s = sbuf("wb_s", [P, S], U8)
-        z_g = sbuf("z_g", [P, S, PACK], BF16)
-        z_w = sbuf("z_w", [P, S], U32)
-        z_s = sbuf("z_s", [P, S], U8)
-        a = [sbuf("a%d" % t, [P, S], F32) for t in range(PACK)]
-        a3 = {}
-        a_ps = {}
-        both = [sbuf("both%d" % t, [P, S], F32) for t in range(PACK)]
-        res = sbuf("res", [P, PACK, S], F32)
-        res_g = sbuf("res_g", [P, S, PACK], BF16)
-        res_w = sbuf("res_w", [P, S], I32)
-        res_s = sbuf("res_s", [P, S], U8)
-        out_rows = out_0.rearrange("(p t) j -> p t j", t=PACK)
-        out_words = out_1[0].rearrange("p c r -> p (c r)").bitcast(I32)
-
-        def a_product(t):
-            a_ps[t] = bank("a_ps%d" % t, "g%d" % t, [P, S])
-            product(a_ps[t], cand_w, cand_s, t, z_w, z_s)
-
-        def a_copy(t, on_scalar):
-            if on_scalar:
-                nc.scalar.activation(a[t][:], a_ps[t][:], ACT.Copy, scale=0.03125)
-            else:
-                nc.vector.tensor_scalar(a[t][:], a_ps[t][:], 0.03125, None, ALU.mult)
-
-        def fetch_n3(t, h):
-            if h == 0 and t < 2:
-                a3[t] = sbuf("a3_%d" % t, [P, S], F32, "fetched%d" % t)
-            if h == 0 and t == 2:
-                a3["late"] = sbuf("a3_late", [P, 2, S], F32, "late")
-                a3[2], a3[3] = a3["late"][:, 0, :], a3["late"][:, 1, :]
-            nc.scalar.activation(a3[t][:, halves[h]], a[t][:].indirect(n3_t[:, 16 * h : 16 * h + 16]), ACT.Copy)
-
-        def finish(t, cols):
-            (nc.gpsimd if t<2 else nc.vector).tensor_tensor(both[t][:, cols], a[t][:, cols], a3[t][:, cols], ALU.add)
-            nc.vector.scalar_tensor_tensor(res[:, t, cols], gate_ps[t][:, cols], 1.0, both[t][:, cols], ALU.add, ALU.mult)
-
-        def store(t):
-            nc.sync.dma_start(out_rows[:, t, :], res[:, t, :])
-
-        def round_pair(u, cols):
-            pair = slice(2 * u, 2 * u + 2)
-            nc.vector.tensor_copy(res_g[:, cols, pair], res[:, pair, cols].rearrange("p t c -> p c t"))
-
-        def planes(cols):
-            round_pair(1, cols)
-            quantize(res_w, res_s, res_g, cols)
-            nc.sync.dma_start(out_words[:, cols], res_w[:, cols])
-
-        for t in range(PACK):
-            fetch_n1(t, True)
-            larger(t)
-        for t in range(PACK):
-            put_n1(t)
-        cb_s = pick_scales("cb_s", cb_t, True)
-        cb_w = pick_words("cb_w", cb_t, True)
-        interleave(wb_g, wb_raw, whole)
-        quantize(wb_w, wb_s, wb_g, whole)
-        for t in range(PACK):
-            b_product(t)
-        cand_s = pick_scales("cand_s", cand_t, True)
-        cand_w = pick_words("cand_w", cand_t, True)
-        for t in range(2):
-            b_copy(t, False)
-        for t in range(2, PACK):
-            b_copy(t, True)
-        for t in range(3):
+        for t in range(LAST):
             weigh(t, whole)
         for cols in halves:
-            weigh(3, cols)
+            weigh(LAST, cols)
         for cols in halves:
             nc.vector.tensor_copy(
-                z_g[:, cols, :].bitcast(I32),
-                z_pairs[:, :, cols, :].bitcast(I32).rearrange("p u c o -> p c (u o)"),
+                z_g[:, cols, :].bitcast(I32), z_pairs[:, :, cols, :].bitcast(I32).rearrange("p u c o -> p c (u o)")
             )
         for cols in halves:
             quantize(z_w, z_s, z_g, cols)
-        fetch_n4(0, True)
+
+        sum_ps = {}
+        tanh_turned = [sbuf("tanh_turned%d" % t, [P, S], F32) for t in range(PACK)]
+        gate_ps = {}
+
+        def add_partner(t, b4, on_scalar):
+            for h in range(2):
+                window = b[t][:].indirect(n4_t[:, LIST_HALF * h : LIST_HALF * (h + 1)])
+                if on_scalar:
+                    nc.scalar.activation(b4[:, halves[h]], window, ACT.Copy)
+                else:
+                    nc.vector.tensor_copy(b4[:, halves[h]], window)
+            sum_ps[t] = bank("sum_ps", "right", t)
+            for cols in quarters:
+                nc.tensor.matmul(sum_ps[t][:, cols], b[t][:, cols], ident[:], start=True, stop=False, is_transpose=True)
+                nc.tensor.matmul(sum_ps[t][:, cols], b4[:, cols], ident[:], start=False, stop=True, is_transpose=True)
+
+        def gate(t):
+            nc.scalar.activation(tanh_turned[t][:], sum_ps[t][:], ACT.Tanh, scale=0.5)
+
+        def turn_back(t):
+            gate_ps[t] = bank("gate_ps", "left", t)
+            for cols in quarters:
+                nc.tensor.transpose(gate_ps[t][:, cols], tanh_turned[t][:, cols], ident[:])
+
+        add_partner(0, sbuf("b4_0", [P, S], F32, "fetched0"), True)
         gate(0)
 
+        a_wide = [sbuf("a%d" % t, [P, S + SPARE], F32) for t in range(LAST)]
+        for tile in a_wide:
+            nc.gpsimd.memset(tile[:, S:], 0.0)
+        a = [tile[:, :S] for tile in a_wide] + [sbuf("a_last", [P, S], F32)[:]]
+        a_ps = [bank("a_ps", "left", t) for t in range(PACK)]
         for t in range(PACK):
-            a_product(t)
-        for t in range(PACK):
-            a_copy(t, t<2)
-            if t == 0:
-                turn_back(0)
-                fetch_n4(1, False)
-            if t in (0, 1):
-                fetch_n4((0, 1).index(t) + 2, False)
-        for t in range(PACK):
+            product(a_ps[t], t, cand_w, cand_s, z_w, z_s)
+
+        def a_copy(t):
+            if t < A_ON_SCALAR:
+                nc.scalar.activation(a[t], a_ps[t][:], ACT.Copy, scale=A_SCALE)
+            else:
+                nc.vector.tensor_scalar(a[t], a_ps[t][:], A_SCALE, None, ALU.mult)
+
+        a_copy(0)
+        turn_back(0)
+        add_partner(1, sbuf("b4_1", [P, S], F32, "fetched1"), False)
+        b4_23 = sbuf("b4_23", [P, 2, S], F32, "fetched23")
+        add_partner(2, b4_23[:, 0, :], False)
+        a_copy(1)
+        add_partner(3, b4_23[:, 1, :], False)
+        a_copy(2)
+        a_copy(3)
+
+        a3 = [sbuf("a3_%d" % t, [P, S], F32, "fetched%d" % t) for t in range(2)]
+        a3_23 = sbuf("a3_23", [P, 2, S], F32, "fetched23")
+        a3 = a3 + [a3_23[:, 0, :], a3_23[:, 1, :]]
+        both = [sbuf("both%d" % t, [P, S], F32) for t in range(PACK)]
+        res = sbuf("res", [P, PACK, S], F32)
+        out_rows = out_0.rearrange("(p t) j -> p t j", t=PACK)
+
+        def finish(t, cols):
+            adder = nc.gpsimd if t < ADD_ON_GPSIMD else nc.vector
+            adder.tensor_tensor(both[t][:, cols], a[t][:, cols], a3[t][:, cols], ALU.add)
+            nc.vector.scalar_tensor_tensor(res[:, t, cols], gate_ps[t][:, cols], 1.0, both[t][:, cols], ALU.add, ALU.mult)
+
+        for t in range(LAST):
             if t > 0:
                 gate(t)
                 turn_back(t)
-            fetch_n3(t, 0)
-            fetch_n3(t, 1)
-            if t < 3:
-                finish(t, whole)
-                store(t)
+            nc.scalar.activation(a3[t][:, whole], a_wide[t][:].indirect(n3_t[:]), ACT.Copy)
+            finish(t, whole)
+            nc.sync.dma_start(out_rows[:, t, :], res[:, t, :])
+        gate(LAST)
+        turn_back(LAST)
+        for h in range(2):
+            window = a[LAST].indirect(n3_t[:, LIST_HALF * h : LIST_HALF * (h + 1)])
+            nc.scalar.activation(a3[LAST][:, halves[h]], window, ACT.Copy)
+
+        res_g = sbuf("res_g", [P, S, PACK], BF16)
+        res_w = sbuf("res_w", [P, S], I32)
+        res_s = sbuf("res_s", [P, S], U8)
+        out_words = out_1[0].rearrange("p c r -> p (c r)").bitcast(I32)
         nc.scalar.copy(res_g[:, :, 0:2], res[:, 0:2, :].rearrange("p t c -> p c t"))
         for cols in halves:
-            finish(3, cols)
-        store(3)
+            finish(LAST, cols)
+        nc.sync.dma_start(out_rows[:, LAST, :], res[:, LAST, :])
         for cols in halves:
-            planes(cols)
+            nc.vector.tensor_copy(res_g[:, cols, 2:4], res[:, 2:4, cols].rearrange("p t c -> p c t"))
+            quantize(res_w, res_s, res_g, cols)
+            nc.sync.dma_start(out_words[:, cols], res_w[:, cols])
         for q in range(4):
             queue = nc.sync if q % 2 else nc.scalar
             queue.dma_start(out_2[0, 4 * q : 4 * q + 4, :].bitcast(I32), res_s[32 * q : 32 * q + 4, :].bitcast(I32))

@@ -57,7 +57,7 @@ def tile_picked_cdswtriebfill_none_po_kernel(
             for q in range(4):
                 nc.sync.dma_start(tile[32 * q : 32 * q + 4, :].bitcast(I32), src[0, 4 * q : 4 * q + 4, :].bitcast(I32))
 
-        x_w = sbuf("x_w", [P, T], I32)
+        x_w = sbuf("x_w", [P, T], I32, "x_words_then_fetched1")
         x_s = sbuf("x_s", [P, T], U8)
         w1_w = sbuf("w1_w", [P, S], I32)
         w1_s = sbuf("w1_s", [P, S], U8, "w1_scales_then_cb_words")
@@ -130,7 +130,7 @@ def tile_picked_cdswtriebfill_none_po_kernel(
         y = [sbuf("y%d" % t, [P, S], F32) for t in range(PACK)]
         pa = sbuf("pa", [P, PACK, W], F32)
         pb = sbuf("pb", [P, PACK, W], F32)
-        ra = sbuf("ra", [P, PACK, W], F32, "ra_then_last_b")
+        ra = sbuf("ra", [P, PACK, W], F32)
         for t in range(PACK):
             nc.scalar.activation(y[t][:], y_ps[t][:], ACT.Copy)
             nc.scalar.activation(pa[:, t, :], y[t][:].indirect(n1_t[:]), ACT.Copy)
@@ -152,19 +152,21 @@ def tile_picked_cdswtriebfill_none_po_kernel(
             product(b_ps[t], t, cb_w, cb_s, wb_w, wb_s)
         cand_s = pick_scales("cand_s", cand_t, True)
         cand_w = pick_words("cand_w", cand_t, True)
-        b = [sbuf("b%d" % t, [P, S], F32) for t in range(LAST)]
-        for t in range(LAST):
+        b = [sbuf("b%d" % t, [P, S], F32) for t in range(PACK)]
+        for t in range(PACK):
             nc.vector.tensor_copy(b[t][:], b_ps[t][:])
-        b.append(sbuf("b_last", [P, S], F32, "ra_then_last_b"))
-        nc.scalar.activation(b[LAST][:], b_ps[LAST][:], ACT.Copy)
 
-        z_pairs = sbuf("z_pairs", [P, 2, S, 2], BF16, "fetched1")
+        z_pairs = sbuf("z_pairs", [P, 2, S, 2], BF16, "x_words_then_fetched1")
         z_g = sbuf("z_g", [P, S, PACK], BF16, "fetched23")
         z_w = sbuf("z_w", [P, S], U32)
         z_s = sbuf("z_s", [P, S], U8)
 
         def weigh(t, cols):
-            nc.vector.tensor_scalar(z_pairs[:, t // 2, cols, t % 2], y[t][:, cols], gs_t[:, t : t + 1], None, ALU.mult)
+            paired = z_pairs[:, t // 2, cols, t % 2]
+            if t < 2:
+                nc.gpsimd.tensor_scalar(paired, y[t][:, cols], gs_t[:, t : t + 1], 0.0, ALU.mult, ALU.add)
+            else:
+                nc.vector.tensor_scalar(paired, y[t][:, cols], gs_t[:, t : t + 1], None, ALU.mult)
 
         for t in range(LAST):
             weigh(t, whole)
@@ -220,7 +222,7 @@ def tile_picked_cdswtriebfill_none_po_kernel(
 
         a_copy(0)
         turn_back(0)
-        add_partner(1, sbuf("b4_1", [P, S], F32, "fetched1"), False)
+        add_partner(1, sbuf("b4_1", [P, S], F32, "x_words_then_fetched1"), False)
         b4_23 = sbuf("b4_23", [P, 2, S], F32, "fetched23")
         add_partner(2, b4_23[:, 0, :], False)
         a_copy(1)
@@ -228,9 +230,10 @@ def tile_picked_cdswtriebfill_none_po_kernel(
         a_copy(2)
         a_copy(3)
 
-        a3 = [sbuf("a3_%d" % t, [P, S], F32, "fetched%d" % t) for t in range(2)]
+        a3_0 = sbuf("a3_0", [P, S], F32, "fetched0")
+        a3_1 = sbuf("a3_1", [P, S], F32, "x_words_then_fetched1")
         a3_23 = sbuf("a3_23", [P, 2, S], F32, "fetched23")
-        a3 = a3 + [a3_23[:, 0, :], a3_23[:, 1, :]]
+        a3 = [a3_0, a3_1, a3_23[:, 0, :], a3_23[:, 1, :]]
         both = [sbuf("both%d" % t, [P, S], F32) for t in range(PACK)]
         res = sbuf("res", [P, PACK, S], F32)
         out_rows = out_0.rearrange("(p t) j -> p t j", t=PACK)

from contextlib import ExitStack

import concourse.mybir as mybir
from concourse.masks import make_identity

F32 = mybir.dt.float32
BF16 = mybir.dt.bfloat16
I32 = mybir.dt.int32
U32 = mybir.dt.uint32
U16 = mybir.dt.uint16
U8 = mybir.dt.uint8
FP8X4 = mybir.dt.float8_e4m3fn_x4
ACT = mybir.ActivationFunctionType
ALU = mybir.AluOpType

P = 128
PACK = 4
T = 2048
S = 512
W = 256
LIST_HALF = 16
SPARE = 16
A_SCALE = 0.0625 * 0.5
LAST = PACK - 1
A_ON_SCALAR = 2
ADD_ON_GPSIMD = 2
FLOPS = 3 * 2 * 512 * 512 * 512


def tile_picked_cdswtriebfill_none_po_kernel(
    tc, x_words, x_scales, w1_words, w1_scales, gs, wb, offs, n1, n2, cand, cb, n3, n4, out_0, out_1, out_2
):
    nc = tc.nc
    whole = slice(0, S)
    halves = [slice(h * W, (h + 1) * W) for h in range(2)]
    quarters = [slice(q * P, (q + 1) * P) for q in range(4)]

    with ExitStack() as ctx:
        keep = ctx.enter_context(tc.tile_pool(name="keep", bufs=1))
        psum = ctx.enter_context(tc.psum_pool(name="psum", bufs=1))

        def sbuf(name, shape, dtype, buffer=""):
            return keep.tile(shape, dtype, name=name, tag=buffer, align_bytes=64)

        def bank(name, side, t):
            return psum.tile([P, S], F32, name="%s%d" % (name, t), tag="%s%d" % (side, t))

        def load_list(name, src):
            tile = keep.tile(list(src.shape), U16, name=name)
            nc.sync.dma_start(tile[:], src)
            return tile

        def load_words(tile, src):
            nc.sync.dma_start(tile[:], src[0].rearrange("p c r -> p (c r)").bitcast(I32))

        def load_scale_rows(tile, src):
            for q in range(4):
                nc.sync.dma_start(tile[32 * q : 32 * q + 4, :].bitcast(I32), src[0, 4 * q : 4 * q + 4, :].bitcast(I32))

        x_w = sbuf("x_w", [P, T], I32, "x_words_then_fetched1")
        x_s = sbuf("x_s", [P, T], U8)
        w1_w = sbuf("w1_w", [P, S], I32)
        w1_s = sbuf("w1_s", [P, S], U8, "w1_scales_then_cb_words")
        nc.gpsimd.memset(x_s[:].bitcast(I32), 0)
        nc.gpsimd.memset(w1_s[:].bitcast(I32), 0)
        load_words(w1_w, w1_words)
        load_scale_rows(x_s, x_scales)
        offs_t = load_list("offs_t", offs)
        cb_t = load_list("cb_t", cb)
        load_words(x_w, x_words)
        load_scale_rows(w1_s, w1_scales)
        n1_t = load_list("n1_t", n1)
        wb_raw = sbuf("wb_raw", [P, PACK, S], F32)
        nc.sync.dma_start(wb_raw[:], wb.rearrange("(p j) w -> p j w", j=PACK))
        n2_t = load_list("n2_t", n2)
        cand_t = load_list("cand_t", cand)
        gs_t = sbuf("gs_t", [P, PACK], F32)
        nc.sync.dma_start(gs_t[:], gs.rearrange("(p t) o -> p (t o)", t=PACK))
        n4_t = load_list("n4_t", n4)
        n3_t = load_list("n3_t", n3)

        ident = sbuf("ident", [P, P], F32)
        make_identity(nc, ident[:])

        def dealt(ap):
            return ap.rearrange("p (t m) -> p m t", t=PACK)

        def deal(name, src, dtype):
            tile = sbuf(name, [P, S], dtype)
            nc.vector.tensor_copy(dealt(tile[:]), src[:].rearrange("p (m t) -> p m t", t=PACK))
            return tile

        def pick_words(name, picks, stationary, buffer=""):
            tile = sbuf(name, [P, S], U32, buffer)
            nc.vector.tensor_copy(dealt(tile[:]) if stationary else tile[:], x_w[:].bitcast(U32).indirect(picks[:]))
            return tile

        def pick_scales(name, picks, stationary):
            tile = sbuf(name, [P, S], U8)
            nc.vector.tensor_copy(dealt(tile[:]) if stationary else tile[:], x_s[:].indirect(picks[:]))
            return tile

        def product(out, t, left_w, left_s, right_w, right_s):
            nc.tensor.matmul_mx(
                out=out[:],
                lhsT=left_w[:, quarters[t]].bitcast(FP8X4),
                lhsT_scale=left_s[:, quarters[t]],
                rhs=right_w[:].bitcast(FP8X4),
                rhs_scale=right_s[:],
                start=True,
                stop=True,
            )

        def quantize(words, scales, grouped, cols):
            nc.vector.quantize_mx(
                out=words[:, cols].bitcast(FP8X4),
                scales=scales[:, cols],
                in_=grouped[:, cols, :].rearrange("p c t -> p (c t)"),
            )

        xq_s = pick_scales("xq_s", offs_t, False)
        w1d_w = deal("w1d_w", w1_w, I32)
        cb_s = pick_scales("cb_s", cb_t, True)
        xq_w = pick_words("xq_w", offs_t, False)
        w1d_s = deal("w1d_s", w1_s, U8)
        y_ps = [bank("y_ps", "left", t) for t in range(PACK)]
        for t in range(PACK):
            product(y_ps[t], t, w1d_w, w1d_s, xq_w, xq_s)

        y = [sbuf("y%d" % t, [P, S], F32) for t in range(PACK)]
        pa = sbuf("pa", [P, PACK, W], F32)
        pb = sbuf("pb", [P, PACK, W], F32)
        ra = sbuf("ra", [P, PACK, W], F32)
        for t in range(PACK):
            nc.scalar.activation(y[t][:], y_ps[t][:], ACT.Copy)
            nc.scalar.activation(pa[:, t, :], y[t][:].indirect(n1_t[:]), ACT.Copy)
            nc.vector.tensor_copy(pb[:, t, :], y[t][:].indirect(n2_t[:]))
            nc.vector.tensor_tensor(ra[:, t, :], pa[:, t, :], pb[:, t, :], ALU.max)
        for t in range(PACK):
            nc.scalar.activation(y[t][:].indirect(n1_t[:]), ra[:, t, :], ACT.Copy)

        cb_w = pick_words("cb_w", cb_t, True, "w1_scales_then_cb_words")
        wb_g = sbuf("wb_g", [P, S, PACK], BF16)
        wb_w = sbuf("wb_w", [P, S], U32)
        wb_s = sbuf("wb_s", [P, S], U8)
        nc.vector.tensor_copy(
            wb_g[:].rearrange("p (c i) t -> p c t i", i=4), wb_raw[:].rearrange("p t (c i) -> p c t i", i=4)
        )
        quantize(wb_w, wb_s, wb_g, whole)
        b_ps = [bank("b_ps", "right", t) for t in range(PACK)]
        for t in range(PACK):
            product(b_ps[t], t, cb_w, cb_s, wb_w, wb_s)
        cand_s = pick_scales("cand_s", cand_t, True)
        cand_w = pick_words("cand_w", cand_t, True)
        b = [sbuf("b%d" % t, [P, S], F32) for t in range(PACK)]
        for t in range(PACK):
            nc.vector.tensor_copy(b[t][:], b_ps[t][:])

        z_pairs = sbuf("z_pairs", [P, 2, S, 2], BF16, "x_words_then_fetched1")
        z_g = sbuf("z_g", [P, S, PACK], BF16, "fetched23")
        z_w = sbuf("z_w", [P, S], U32)
        z_s = sbuf("z_s", [P, S], U8)

        def weigh(t, cols):
            paired = z_pairs[:, t // 2, cols, t % 2]
            if t < 2:
                nc.gpsimd.tensor_scalar(paired, y[t][:, cols], gs_t[:, t : t + 1], 0.0, ALU.mult, ALU.add)
            else:
                nc.vector.tensor_scalar(paired, y[t][:, cols], gs_t[:, t : t + 1], None, ALU.mult)

        for t in range(LAST):
            weigh(t, whole)
        for cols in halves:
            weigh(LAST, cols)
        for cols in halves:
            nc.vector.tensor_copy(
                z_g[:, cols, :].bitcast(I32), z_pairs[:, :, cols, :].bitcast(I32).rearrange("p u c o -> p c (u o)")
            )
        for cols in halves:
            quantize(z_w, z_s, z_g, cols)

        sum_ps = {}
        tanh_turned = [sbuf("tanh_turned%d" % t, [P, S], F32) for t in range(PACK)]
        gate_ps = {}

        def add_partner(t, b4, on_scalar):
            for h in range(2):
                window = b[t][:].indirect(n4_t[:, LIST_HALF * h : LIST_HALF * (h + 1)])
                if on_scalar:
                    nc.scalar.activation(b4[:, halves[h]], window, ACT.Copy)
                else:
                    nc.vector.tensor_copy(b4[:, halves[h]], window)
            sum_ps[t] = bank("sum_ps", "right", t)
            for cols in quarters:
                nc.tensor.matmul(sum_ps[t][:, cols], b[t][:, cols], ident[:], start=True, stop=False, is_transpose=True)
                nc.tensor.matmul(sum_ps[t][:, cols], b4[:, cols], ident[:], start=False, stop=True, is_transpose=True)

        def gate(t):
            nc.scalar.activation(tanh_turned[t][:], sum_ps[t][:], ACT.Tanh, scale=0.5)

        def turn_back(t):
            gate_ps[t] = bank("gate_ps", "left", t)
            for cols in quarters:
                nc.tensor.transpose(gate_ps[t][:, cols], tanh_turned[t][:, cols], ident[:])

        add_partner(0, sbuf("b4_0", [P, S], F32, "fetched0"), True)
        gate(0)

        a_wide = [sbuf("a%d" % t, [P, S + SPARE], F32) for t in range(LAST)]
        for tile in a_wide:
            nc.gpsimd.memset(tile[:, S:], 0.0)
        a = [tile[:, :S] for tile in a_wide] + [sbuf("a_last", [P, S], F32)[:]]
        a_ps = [bank("a_ps", "left", t) for t in range(PACK)]
        for t in range(PACK):
            product(a_ps[t], t, cand_w, cand_s, z_w, z_s)

        def a_copy(t):
            if t < A_ON_SCALAR:
                nc.scalar.activation(a[t], a_ps[t][:], ACT.Copy, scale=A_SCALE)
            else:
                nc.vector.tensor_scalar(a[t], a_ps[t][:], A_SCALE, None, ALU.mult)

        a_copy(0)
        turn_back(0)
        add_partner(1, sbuf("b4_1", [P, S], F32, "x_words_then_fetched1"), False)
        b4_23 = sbuf("b4_23", [P, 2, S], F32, "fetched23")
        add_partner(2, b4_23[:, 0, :], False)
        a_copy(1)
        add_partner(3, b4_23[:, 1, :], False)
        a_copy(2)
        a_copy(3)

        a3_0 = sbuf("a3_0", [P, S], F32, "fetched0")
        a3_1 = sbuf("a3_1", [P, S], F32, "x_words_then_fetched1")
        a3_23 = sbuf("a3_23", [P, 2, S], F32, "fetched23")
        a3 = [a3_0, a3_1, a3_23[:, 0, :], a3_23[:, 1, :]]
        both = [sbuf("both%d" % t, [P, S], F32) for t in range(PACK)]
        res = sbuf("res", [P, PACK, S], F32)
        out_rows = out_0.rearrange("(p t) j -> p t j", t=PACK)

        def finish(t, cols):
            adder = nc.gpsimd if t < ADD_ON_GPSIMD else nc.vector
            adder.tensor_tensor(both[t][:, cols], a[t][:, cols], a3[t][:, cols], ALU.add)
            nc.vector.scalar_tensor_tensor(res[:, t, cols], gate_ps[t][:, cols], 1.0, both[t][:, cols], ALU.add, ALU.mult)

        for t in range(LAST):
            if t > 0:
                gate(t)
                turn_back(t)
            nc.scalar.activation(a3[t][:, whole], a_wide[t][:].indirect(n3_t[:]), ACT.Copy)
            finish(t, whole)
            nc.sync.dma_start(out_rows[:, t, :], res[:, t, :])
        gate(LAST)
        turn_back(LAST)
        for h in range(2):
            window = a[LAST].indirect(n3_t[:, LIST_HALF * h : LIST_HALF * (h + 1)])
            nc.scalar.activation(a3[LAST][:, halves[h]], window, ACT.Copy)

        res_g = sbuf("res_g", [P, S, PACK], BF16)
        res_w = sbuf("res_w", [P, S], I32)
        res_s = sbuf("res_s", [P, S], U8)
        out_words = out_1[0].rearrange("p c r -> p (c r)").bitcast(I32)
        nc.scalar.copy(res_g[:, :, 0:2], res[:, 0:2, :].rearrange("p t c -> p c t"))
        for cols in halves:
            finish(LAST, cols)
        nc.sync.dma_start(out_rows[:, LAST, :], res[:, LAST, :])
        for cols in halves:
            nc.vector.tensor_copy(res_g[:, cols, 2:4], res[:, 2:4, cols].rearrange("p t c -> p c t"))
            quantize(res_w, res_s, res_g, cols)
            nc.sync.dma_start(out_words[:, cols], res_w[:, cols])
        for q in range(4):
            queue = nc.sync if q % 2 else nc.scalar
            queue.dma_start(out_2[0, 4 * q : 4 * q + 4, :].bitcast(I32), res_s[32 * q : 32 * q + 4, :].bitcast(I32))
